import numpy as np
import ml_dtypes


def mxq(x, axis, fmt="e4m3"):
    dtype, down = {"e4m3": (ml_dtypes.float8_e4m3fn, 7), "e5m2": (ml_dtypes.float8_e5m2, 14)}[fmt]
    v = np.moveaxis(np.asarray(x, np.float32).astype(ml_dtypes.bfloat16).astype(np.float64), axis, -1)
    blocks = v.reshape(v.shape[:-1] + (-1, 32))
    amax = np.abs(blocks).max(-1, keepdims=True)
    byte = np.maximum(np.where(amax > 0, np.frexp(amax)[1] - 1 + 127, 0) - down, 1)
    scale = np.exp2(byte - 127.0)
    codes = (blocks / scale).astype(np.float32).astype(dtype).astype(np.float64)
    return np.moveaxis((codes * scale).reshape(v.shape), -1, axis)


WIDE = False


def mx_kscale(k):
    if not WIDE:
        return np.ones(k)
    levels = np.array([10, -10, 5, -5, 0])
    if k % 512:
        return np.exp2(np.random.permutation(np.resize(levels, k // 32))).repeat(32)
    a = np.empty((k // 512, 16))
    for p in range(k // 512):
        a[p, :8] = np.random.permutation(np.resize(levels, 8))
        for g in range(8):
            far = levels[np.abs(levels - a[p, g]) >= 10]
            a[p, g + 8] = far[np.random.randint(len(far))]
    return np.exp2(a.ravel()).repeat(32)


def f64(x):
    return np.asarray(x).astype(np.float64)


def striped(idx):
    return np.tile(idx.reshape(-1, 16).T, (8, 1)).astype(np.uint16)


def unstriped(offs):
    return offs[:16].T.reshape(-1).astype(np.int64)


def pack_weight(w):
    k, n = w.shape
    w = f64(np.asarray(w, np.float32).astype(ml_dtypes.bfloat16)).reshape(k // 32, 32, n)
    amax = np.abs(w).max(1)
    byte = np.clip(np.where(amax > 0, np.frexp(amax)[1] - 1 + 127 - 7, 1), 1, 254)
    scaled = (w * np.exp2(127.0 - byte)[:, None, :]).reshape(k, n).astype(np.float32)
    words = np.ascontiguousarray(scaled.reshape(k // 512, 128, 4, n).transpose(0, 1, 3, 2)).astype(ml_dtypes.float8_e4m3fn).view(np.uint8)
    return words, np.ascontiguousarray(byte.astype(np.uint8).reshape(k // 512, 16, n))


def unpack_weight(words, scales):
    g, p, n, _ = words.shape
    vals = np.ascontiguousarray(words).view(ml_dtypes.float8_e4m3fn).astype(np.float64) * np.repeat(np.exp2(scales.astype(np.float64) - 127.0), 8, axis=1)[..., None]
    return vals.transpose(0, 1, 3, 2).reshape(g * 512, n)


K, T, S, N, U = 512, 2048, 512, 128, 1024


def setup_inputs():
    n = np.random.standard_normal
    s = mx_kscale(K)[:, None]
    packed_xT = pack_weight(n((K, T)) * s)
    return {
        "x_words": packed_xT[0],
        "x_scales": packed_xT[1],
        "w1": (n((K, N)) / np.sqrt(K) / s).astype(np.float32),
        "cnt0": (np.random.uniform(0.0, 4.0, (N, U))).astype(np.float32),
        "cnt1": (np.random.uniform(0.0, 4.0, (N, U))).astype(np.float32),
        "cnt2": (np.random.uniform(0.0, 4.0, (N, U))).astype(np.float32),
        "offs": striped(np.random.permutation(T)[:S]),
        "hash0": striped(np.random.permutation(U)[:S]),
        "hash1": striped(np.random.permutation(U)[:S]),
        "hash2": striped(np.random.permutation(U)[:S]),
    }


def reference(x_words, x_scales, w1, cnt0, cnt1, cnt2, offs, hash0, hash1, hash2):
    g0 = f64(cnt0)[:, unstriped(hash0)]
    g1 = f64(cnt1)[:, unstriped(hash1)]
    g2 = f64(cnt2)[:, unstriped(hash2)]
    xq = unpack_weight(x_words, x_scales)[:, unstriped(offs)]
    y = mxq(f64(w1), 0, "e4m3").T @ xq
    inc = np.log(np.exp(y) + 1.0)
    est = np.minimum(np.minimum(g0, g1), g2) + inc
    cnew = np.maximum(g0, est)
    out = f64(cnt0).copy()
    out[:, unstriped(hash0)] = cnew
    return out

@@ -1,0 +1,125 @@
+from contextlib import ExitStack
+
+import concourse.mybir as mybir
+
+K, T, S, N, U = 512, 2048, 512, 128, 1024
+FLOPS = 2 * K * N * S
+
+F32 = mybir.dt.float32
+BF16 = mybir.dt.bfloat16
+I32 = mybir.dt.int32
+U32 = mybir.dt.uint32
+U16 = mybir.dt.uint16
+U8 = mybir.dt.uint8
+FP8X4 = mybir.dt.float8_e4m3fn_x4
+ALU = mybir.AluOpType
+ACT = mybir.ActivationFunctionType
+
+P = 128
+PACK = 4
+LANES = 16
+PIECES = 2
+
+
+def tile_picked_ycms2_put_p_kernel(
+    tc, x_words, x_scales, w1, cnt0, cnt1, cnt2, offs, hash0, hash1, hash2, out
+):
+    nc = tc.nc
+    width = S // PIECES
+    cols = width // LANES
+
+    with ExitStack() as ctx:
+        lists = ctx.enter_context(tc.tile_pool(name="lists", bufs=1))
+        keep = ctx.enter_context(tc.tile_pool(name="keep", bufs=1))
+        psum = ctx.enter_context(tc.psum_pool(name="psum", bufs=1))
+
+        offs_t = lists.tile([P, S // LANES], U16, name="offs_t")
+        h0_t = lists.tile([P, S // LANES], U16, name="h0_t")
+        h1_t = lists.tile([P, S // LANES], U16, name="h1_t")
+        h2_t = lists.tile([P, S // LANES], U16, name="h2_t")
+
+        words = keep.tile([P, T], I32, name="words", align_bytes=64)
+        scales = keep.tile([P, T], U8, name="scales", align_bytes=64)
+        w_raw = keep.tile([P, PACK, N], F32, name="w_raw", align_bytes=64)
+        c0 = keep.tile([P, U], F32, name="c0", align_bytes=64)
+        c1 = keep.tile([P, U], F32, name="c1", align_bytes=64)
+        c2 = keep.tile([P, U], F32, name="c2", align_bytes=64)
+
+        nc.vector.memset(scales[:].bitcast(I32), 0)
+        nc.sync.dma_start(offs_t[:], offs)
+        for q in range(4):
+            nc.scalar.dma_start(
+                scales[32 * q : 32 * q + 4, :].bitcast(I32),
+                x_scales[0, 4 * q : 4 * q + 4, :].bitcast(I32),
+            )
+        nc.sync.dma_start(w_raw[:], w1.rearrange("(p j) n -> p j n", j=PACK))
+        nc.sync.dma_start(words[:], x_words[0].rearrange("p c r -> p (c r)").bitcast(I32))
+        nc.sync.dma_start(h0_t[:], hash0)
+        nc.sync.dma_start(c0[:], cnt0)
+        nc.sync.dma_start(h1_t[:], hash1)
+        nc.sync.dma_start(c1[:], cnt1)
+        nc.sync.dma_start(h2_t[:], hash2)
+        nc.sync.dma_start(c2[:], cnt2)
+
+        w_bf = keep.tile([P, N, PACK], BF16, name="w_bf", align_bytes=64)
+        nc.scalar.activation(w_bf[:], w_raw[:].rearrange("p j n -> p n j"), ACT.Copy)
+        w_codes = keep.tile([P, N], U32, name="w_codes", align_bytes=64)
+        w_scales = keep.tile([P, N], U8, name="w_scales", align_bytes=64)
+
+        x_sc = keep.tile([P, S], U8, name="x_sc", align_bytes=64)
+        nc.vector.tensor_copy(x_sc[:], scales[:].indirect(offs_t[:]))
+
+        x_codes = [keep.tile([P, width], U32, name=f"x_codes{i}", align_bytes=64) for i in range(PIECES)]
+        nc.vector.tensor_copy(x_codes[0][:], words[:].bitcast(U32).indirect(offs_t[:, 0:cols]))
+        nc.vector.quantize_mx(
+            out=w_codes[:].bitcast(FP8X4),
+            scales=w_scales[:],
+            in_=w_bf[:].rearrange("p n j -> p (n j)"),
+        )
+        for i in range(1, PIECES):
+            nc.vector.tensor_copy(x_codes[i][:], words[:].bitcast(U32).indirect(offs_t[:, i * cols : (i + 1) * cols]))
+
+        y = [psum.tile([P, width], F32, name=f"y{i}") for i in range(PIECES)]
+        e = [keep.tile([P, width], F32, name=f"e{i}") for i in range(PIECES)]
+        for i in range(PIECES):
+            nc.tensor.matmul_mx(
+                out=y[i][:],
+                lhsT=w_codes[:].bitcast(FP8X4),
+                lhsT_scale=w_scales[:],
+                rhs=x_codes[i][:].bitcast(FP8X4),
+                rhs_scale=x_sc[:, i * width : (i + 1) * width],
+                start=True,
+                stop=True,
+            )
+            a = keep.tile([P, width], F32, name=f"a{i}")
+            nc.scalar.activation(a[:], y[i][:], ACT.Abs)
+            nc.scalar.activation(e[i][:], a[:], ACT.Exp, scale=-1.0)
+        tail = [keep.tile([P, width], F32, name=f"tail{i}") for i in range(PIECES)]
+        for i in range(PIECES):
+            nc.scalar.activation(tail[i][:], e[i][:], ACT.Ln, bias=1.0)
+
+        g0 = keep.tile([P, S], F32, name="g0")
+        d1 = keep.tile([P, S], F32, name="d1")
+        d2 = keep.tile([P, S], F32, name="d2")
+        nc.vector.tensor_copy(g0[:], c0[:].indirect(h0_t[:]))
+        nc.vector.tensor_tensor(d1[:], c1[:].indirect(h1_t[:]), g0[:], ALU.subtract)
+        nc.vector.tensor_tensor(d2[:], c2[:].indirect(h2_t[:]), g0[:], ALU.subtract)
+
+        gap = [keep.tile([P, width], F32, name=f"gap{i}") for i in range(PIECES)]
+        part = [keep.tile([P, width], F32, name=f"part{i}") for i in range(PIECES)]
+        full = [keep.tile([P, width], F32, name=f"full{i}") for i in range(PIECES)]
+        rise = [keep.tile([P, width], F32, name=f"rise{i}") for i in range(PIECES)]
+        span = [slice(i * width, (i + 1) * width) for i in range(PIECES)]
+        for i in range(PIECES):
+            nc.vector.scalar_tensor_tensor(gap[i][:], d1[:, span[i]], 0.0, d2[:, span[i]], ALU.min, ALU.min)
+        for i in range(PIECES):
+            nc.vector.scalar_tensor_tensor(part[i][:], y[i][:], 0.0, gap[i][:], ALU.max, ALU.add)
+        for i in range(PIECES):
+            nc.vector.tensor_tensor(full[i][:], part[i][:], tail[i][:], ALU.add)
+        for i in range(PIECES):
+            nc.vector.tensor_scalar_max(rise[i][:], full[i][:], 0.0)
+        for i in range(PIECES):
+            nc.vector.tensor_tensor(
+                c0[:].indirect(h0_t[:, i * cols : (i + 1) * cols]), g0[:, span[i]], rise[i][:], ALU.add
+            )
+        nc.sync.dma_start(out, c0[:])

@@ -47,14 +47,14 @@ def tile_picked_ycms2_put_p_kernel(
 
         nc.vector.memset(scales[:].bitcast(I32), 0)
         nc.sync.dma_start(offs_t[:], offs)
+        nc.sync.dma_start(w_raw[:], w1.rearrange("(p j) n -> p j n", j=PACK))
+        nc.sync.dma_start(h0_t[:], hash0)
         for q in range(4):
-            nc.scalar.dma_start(
+            nc.sync.dma_start(
                 scales[32 * q : 32 * q + 4, :].bitcast(I32),
                 x_scales[0, 4 * q : 4 * q + 4, :].bitcast(I32),
             )
-        nc.sync.dma_start(w_raw[:], w1.rearrange("(p j) n -> p j n", j=PACK))
         nc.sync.dma_start(words[:], x_words[0].rearrange("p c r -> p (c r)").bitcast(I32))
-        nc.sync.dma_start(h0_t[:], hash0)
         nc.sync.dma_start(c0[:], cnt0)
         nc.sync.dma_start(h1_t[:], hash1)
         nc.sync.dma_start(c1[:], cnt1)
@@ -100,24 +100,26 @@ def tile_picked_ycms2_put_p_kernel(
 
         g0 = keep.tile([P, S], F32, name="g0")
         d1 = keep.tile([P, S], F32, name="d1")
-        d2 = keep.tile([P, S], F32, name="d2")
         nc.vector.tensor_copy(g0[:], c0[:].indirect(h0_t[:]))
         nc.vector.tensor_tensor(d1[:], c1[:].indirect(h1_t[:]), g0[:], ALU.subtract)
-        nc.vector.tensor_tensor(d2[:], c2[:].indirect(h2_t[:]), g0[:], ALU.subtract)
 
+        span = [slice(i * width, (i + 1) * width) for i in range(PIECES)]
+        d2 = [keep.tile([P, width], F32, name=f"d2{i}") for i in range(PIECES)]
         gap = [keep.tile([P, width], F32, name=f"gap{i}") for i in range(PIECES)]
         part = [keep.tile([P, width], F32, name=f"part{i}") for i in range(PIECES)]
         full = [keep.tile([P, width], F32, name=f"full{i}") for i in range(PIECES)]
         rise = [keep.tile([P, width], F32, name=f"rise{i}") for i in range(PIECES)]
-        span = [slice(i * width, (i + 1) * width) for i in range(PIECES)]
         for i in range(PIECES):
-            nc.vector.scalar_tensor_tensor(gap[i][:], d1[:, span[i]], 0.0, d2[:, span[i]], ALU.min, ALU.min)
+            nc.vector.tensor_tensor(
+                d2[i][:], c2[:].indirect(h2_t[:, i * cols : (i + 1) * cols]), g0[:, span[i]], ALU.subtract
+            )
+        for i in range(PIECES):
+            nc.vector.scalar_tensor_tensor(gap[i][:], d1[:, span[i]], 0.0, d2[i][:], ALU.min, ALU.min)
         for i in range(PIECES):
             nc.vector.scalar_tensor_tensor(part[i][:], y[i][:], 0.0, gap[i][:], ALU.max, ALU.add)
         for i in range(PIECES):
             nc.vector.tensor_tensor(full[i][:], part[i][:], tail[i][:], ALU.add)
-        for i in range(PIECES):
-            nc.vector.tensor_scalar_max(rise[i][:], full[i][:], 0.0)
+            nc.scalar.activation(rise[i][:], full[i][:], ACT.Relu)
         for i in range(PIECES):
             nc.vector.tensor_tensor(
                 c0[:].indirect(h0_t[:, i * cols : (i + 1) * cols]), g0[:, span[i]], rise[i][:], ALU.add

@@ -46,21 +46,23 @@ def tile_picked_ycms2_put_p_kernel(
         c2 = keep.tile([P, U], F32, name="c2", align_bytes=64)
 
         nc.vector.memset(scales[:].bitcast(I32), 0)
+        nc.sync.dma_start(h0_t[:], hash0)
+        nc.sync.dma_start(c0[:], cnt0)
         nc.sync.dma_start(offs_t[:], offs)
         nc.sync.dma_start(w_raw[:], w1.rearrange("(p j) n -> p j n", j=PACK))
-        nc.sync.dma_start(h0_t[:], hash0)
         for q in range(4):
             nc.sync.dma_start(
                 scales[32 * q : 32 * q + 4, :].bitcast(I32),
                 x_scales[0, 4 * q : 4 * q + 4, :].bitcast(I32),
             )
         nc.sync.dma_start(words[:], x_words[0].rearrange("p c r -> p (c r)").bitcast(I32))
-        nc.sync.dma_start(c0[:], cnt0)
         nc.sync.dma_start(h1_t[:], hash1)
         nc.sync.dma_start(c1[:], cnt1)
         nc.sync.dma_start(h2_t[:], hash2)
         nc.sync.dma_start(c2[:], cnt2)
 
+        g0 = keep.tile([P, S], F32, name="g0")
+        nc.vector.tensor_copy(g0[:], c0[:].indirect(h0_t[:]))
         w_bf = keep.tile([P, N, PACK], BF16, name="w_bf", align_bytes=64)
         nc.scalar.activation(w_bf[:], w_raw[:].rearrange("p j n -> p n j"), ACT.Copy)
         w_codes = keep.tile([P, N], U32, name="w_codes", align_bytes=64)
@@ -98,9 +100,7 @@ def tile_picked_ycms2_put_p_kernel(
         for i in range(PIECES):
             nc.scalar.activation(tail[i][:], e[i][:], ACT.Ln, bias=1.0)
 
-        g0 = keep.tile([P, S], F32, name="g0")
         d1 = keep.tile([P, S], F32, name="d1")
-        nc.vector.tensor_copy(g0[:], c0[:].indirect(h0_t[:]))
         nc.vector.tensor_tensor(d1[:], c1[:].indirect(h1_t[:]), g0[:], ALU.subtract)
 
         span = [slice(i * width, (i + 1) * width) for i in range(PIECES)]
@@ -108,7 +108,7 @@ def tile_picked_ycms2_put_p_kernel(
         gap = [keep.tile([P, width], F32, name=f"gap{i}") for i in range(PIECES)]
         part = [keep.tile([P, width], F32, name=f"part{i}") for i in range(PIECES)]
         full = [keep.tile([P, width], F32, name=f"full{i}") for i in range(PIECES)]
-        rise = [keep.tile([P, width], F32, name=f"rise{i}") for i in range(PIECES)]
+        rise = keep.tile([P, S], F32, name="rise")
         for i in range(PIECES):
             nc.vector.tensor_tensor(
                 d2[i][:], c2[:].indirect(h2_t[:, i * cols : (i + 1) * cols]), g0[:, span[i]], ALU.subtract
@@ -119,9 +119,7 @@ def tile_picked_ycms2_put_p_kernel(
             nc.vector.scalar_tensor_tensor(part[i][:], y[i][:], 0.0, gap[i][:], ALU.max, ALU.add)
         for i in range(PIECES):
             nc.vector.tensor_tensor(full[i][:], part[i][:], tail[i][:], ALU.add)
-            nc.scalar.activation(rise[i][:], full[i][:], ACT.Relu)
         for i in range(PIECES):
-            nc.vector.tensor_tensor(
-                c0[:].indirect(h0_t[:, i * cols : (i + 1) * cols]), g0[:, span[i]], rise[i][:], ALU.add
-            )
+            nc.vector.tensor_scalar_max(rise[:, span[i]], full[i][:], 0.0)
+        nc.vector.tensor_tensor(c0[:].indirect(h0_t[:]), g0[:], rise[:], ALU.add)
         nc.sync.dma_start(out, c0[:])

@@ -17,109 +17,120 @@ ACT = mybir.ActivationFunctionType
 
 P = 128
 PACK = 4
-LANES = 16
-PIECES = 2
+QUADRANT = 32
+SCALE_ROWS = 4
+ENTRIES_PER_COLUMN = 16
+HALVES = 2
+WIDTH = S // HALVES
 
 
 def tile_picked_ycms2_put_p_kernel(
     tc, x_words, x_scales, w1, cnt0, cnt1, cnt2, offs, hash0, hash1, hash2, out
 ):
     nc = tc.nc
-    width = S // PIECES
-    cols = width // LANES
+    list_columns = S // ENTRIES_PER_COLUMN
+    half_columns = WIDTH // ENTRIES_PER_COLUMN
+    entries = [slice(h * WIDTH, (h + 1) * WIDTH) for h in range(HALVES)]
+    columns = [slice(h * half_columns, (h + 1) * half_columns) for h in range(HALVES)]
 
     with ExitStack() as ctx:
         lists = ctx.enter_context(tc.tile_pool(name="lists", bufs=1))
         keep = ctx.enter_context(tc.tile_pool(name="keep", bufs=1))
         psum = ctx.enter_context(tc.psum_pool(name="psum", bufs=1))
 
-        offs_t = lists.tile([P, S // LANES], U16, name="offs_t")
-        h0_t = lists.tile([P, S // LANES], U16, name="h0_t")
-        h1_t = lists.tile([P, S // LANES], U16, name="h1_t")
-        h2_t = lists.tile([P, S // LANES], U16, name="h2_t")
+        def halves(name, dtype):
+            return [keep.tile([P, WIDTH], dtype, name=f"{name}{h}", align_bytes=64) for h in range(HALVES)]
 
-        words = keep.tile([P, T], I32, name="words", align_bytes=64)
-        scales = keep.tile([P, T], U8, name="scales", align_bytes=64)
+        idx_list = lists.tile([P, list_columns], U16, name="idx_list")
+        h0_list = lists.tile([P, list_columns], U16, name="h0_list")
+        h1_list = lists.tile([P, list_columns], U16, name="h1_list")
+        h2_list = lists.tile([P, list_columns], U16, name="h2_list")
+
+        all_words = keep.tile([P, T], I32, name="all_words", align_bytes=64)
+        all_scales = keep.tile([P, T], U8, name="all_scales", align_bytes=64)
         w_raw = keep.tile([P, PACK, N], F32, name="w_raw", align_bytes=64)
-        c0 = keep.tile([P, U], F32, name="c0", align_bytes=64)
-        c1 = keep.tile([P, U], F32, name="c1", align_bytes=64)
-        c2 = keep.tile([P, U], F32, name="c2", align_bytes=64)
+        row0 = keep.tile([P, U], F32, name="row0", align_bytes=64)
+        row1 = keep.tile([P, U], F32, name="row1", align_bytes=64)
+        row2 = keep.tile([P, U], F32, name="row2", align_bytes=64)
 
-        nc.vector.memset(scales[:].bitcast(I32), 0)
-        nc.sync.dma_start(h0_t[:], hash0)
-        nc.sync.dma_start(c0[:], cnt0)
-        nc.sync.dma_start(offs_t[:], offs)
-        nc.sync.dma_start(w_raw[:], w1.rearrange("(p j) n -> p j n", j=PACK))
-        for q in range(4):
+        nc.vector.memset(all_scales[:].bitcast(I32), 0)
+
+        nc.sync.dma_start(idx_list[:], offs)
+        nc.sync.dma_start(w_raw[:], w1.rearrange("(p t) n -> p t n", t=PACK))
+        nc.sync.dma_start(h0_list[:], hash0)
+        for q in range(P // QUADRANT):
             nc.sync.dma_start(
-                scales[32 * q : 32 * q + 4, :].bitcast(I32),
-                x_scales[0, 4 * q : 4 * q + 4, :].bitcast(I32),
+                all_scales[QUADRANT * q : QUADRANT * q + SCALE_ROWS, :].bitcast(I32),
+                x_scales[0, SCALE_ROWS * q : SCALE_ROWS * (q + 1), :].bitcast(I32),
             )
-        nc.sync.dma_start(words[:], x_words[0].rearrange("p c r -> p (c r)").bitcast(I32))
-        nc.sync.dma_start(h1_t[:], hash1)
-        nc.sync.dma_start(c1[:], cnt1)
-        nc.sync.dma_start(h2_t[:], hash2)
-        nc.sync.dma_start(c2[:], cnt2)
+        nc.sync.dma_start(all_words[:], x_words[0].rearrange("p c t -> p (c t)").bitcast(I32))
+        nc.sync.dma_start(row0[:], cnt0)
+        nc.sync.dma_start(h1_list[:], hash1)
+        nc.sync.dma_start(row1[:], cnt1)
+        nc.sync.dma_start(h2_list[:], hash2)
+        nc.sync.dma_start(row2[:], cnt2)
 
-        g0 = keep.tile([P, S], F32, name="g0")
-        nc.vector.tensor_copy(g0[:], c0[:].indirect(h0_t[:]))
-        w_bf = keep.tile([P, N, PACK], BF16, name="w_bf", align_bytes=64)
-        nc.scalar.activation(w_bf[:], w_raw[:].rearrange("p j n -> p n j"), ACT.Copy)
-        w_codes = keep.tile([P, N], U32, name="w_codes", align_bytes=64)
+        w_bf16 = keep.tile([P, N, PACK], BF16, name="w_bf16", align_bytes=64)
+        w_words = keep.tile([P, N], U32, name="w_words", align_bytes=64)
         w_scales = keep.tile([P, N], U8, name="w_scales", align_bytes=64)
-
-        x_sc = keep.tile([P, S], U8, name="x_sc", align_bytes=64)
-        nc.vector.tensor_copy(x_sc[:], scales[:].indirect(offs_t[:]))
-
-        x_codes = [keep.tile([P, width], U32, name=f"x_codes{i}", align_bytes=64) for i in range(PIECES)]
-        nc.vector.tensor_copy(x_codes[0][:], words[:].bitcast(U32).indirect(offs_t[:, 0:cols]))
+        nc.scalar.activation(w_bf16[:], w_raw[:].rearrange("p t n -> p n t"), ACT.Copy)
         nc.vector.quantize_mx(
-            out=w_codes[:].bitcast(FP8X4),
+            out=w_words[:].bitcast(FP8X4),
             scales=w_scales[:],
-            in_=w_bf[:].rearrange("p n j -> p (n j)"),
+            in_=w_bf16[:].rearrange("p n t -> p (n t)"),
         )
-        for i in range(1, PIECES):
-            nc.vector.tensor_copy(x_codes[i][:], words[:].bitcast(U32).indirect(offs_t[:, i * cols : (i + 1) * cols]))
 
-        y = [psum.tile([P, width], F32, name=f"y{i}") for i in range(PIECES)]
-        e = [keep.tile([P, width], F32, name=f"e{i}") for i in range(PIECES)]
-        for i in range(PIECES):
+        picked_scales = keep.tile([P, S], U8, name="picked_scales", align_bytes=64)
+        picked_words = halves("picked_words", U32)
+        nc.vector.tensor_copy(picked_scales[:], all_scales[:].indirect(idx_list[:]))
+        for h in range(HALVES):
+            nc.vector.tensor_copy(picked_words[h][:], all_words[:].bitcast(U32).indirect(idx_list[:, columns[h]]))
+
+        y = [psum.tile([P, WIDTH], F32, name=f"y{h}") for h in range(HALVES)]
+        y_abs = halves("y_abs", F32)
+        decay = halves("decay", F32)
+        log_term = halves("log_term", F32)
+        for h in range(HALVES):
             nc.tensor.matmul_mx(
-                out=y[i][:],
-                lhsT=w_codes[:].bitcast(FP8X4),
+                out=y[h][:],
+                lhsT=w_words[:].bitcast(FP8X4),
                 lhsT_scale=w_scales[:],
-                rhs=x_codes[i][:].bitcast(FP8X4),
-                rhs_scale=x_sc[:, i * width : (i + 1) * width],
+                rhs=picked_words[h][:].bitcast(FP8X4),
+                rhs_scale=picked_scales[:, entries[h]],
                 start=True,
                 stop=True,
             )
-            a = keep.tile([P, width], F32, name=f"a{i}")
-            nc.scalar.activation(a[:], y[i][:], ACT.Abs)
-            nc.scalar.activation(e[i][:], a[:], ACT.Exp, scale=-1.0)
-        tail = [keep.tile([P, width], F32, name=f"tail{i}") for i in range(PIECES)]
-        for i in range(PIECES):
-            nc.scalar.activation(tail[i][:], e[i][:], ACT.Ln, bias=1.0)
+            nc.scalar.activation(y_abs[h][:], y[h][:], ACT.Abs)
+            nc.scalar.activation(decay[h][:], y_abs[h][:], ACT.Exp, scale=-1.0)
+        for h in range(HALVES):
+            nc.scalar.activation(log_term[h][:], decay[h][:], ACT.Ln, bias=1.0)
 
-        d1 = keep.tile([P, S], F32, name="d1")
-        nc.vector.tensor_tensor(d1[:], c1[:].indirect(h1_t[:]), g0[:], ALU.subtract)
-
-        span = [slice(i * width, (i + 1) * width) for i in range(PIECES)]
-        d2 = [keep.tile([P, width], F32, name=f"d2{i}") for i in range(PIECES)]
-        gap = [keep.tile([P, width], F32, name=f"gap{i}") for i in range(PIECES)]
-        part = [keep.tile([P, width], F32, name=f"part{i}") for i in range(PIECES)]
-        full = [keep.tile([P, width], F32, name=f"full{i}") for i in range(PIECES)]
-        rise = keep.tile([P, S], F32, name="rise")
-        for i in range(PIECES):
+        g0 = keep.tile([P, S], F32, name="g0")
+        diff1 = halves("diff1", F32)
+        diff2 = halves("diff2", F32)
+        for h in range(HALVES):
+            nc.vector.tensor_copy(g0[:, entries[h]], row0[:].indirect(h0_list[:, columns[h]]))
+        for h in range(HALVES):
             nc.vector.tensor_tensor(
-                d2[i][:], c2[:].indirect(h2_t[:, i * cols : (i + 1) * cols]), g0[:, span[i]], ALU.subtract
+                diff1[h][:], row1[:].indirect(h1_list[:, columns[h]]), g0[:, entries[h]], ALU.subtract
             )
-        for i in range(PIECES):
-            nc.vector.scalar_tensor_tensor(gap[i][:], d1[:, span[i]], 0.0, d2[i][:], ALU.min, ALU.min)
-        for i in range(PIECES):
-            nc.vector.scalar_tensor_tensor(part[i][:], y[i][:], 0.0, gap[i][:], ALU.max, ALU.add)
-        for i in range(PIECES):
-            nc.vector.tensor_tensor(full[i][:], part[i][:], tail[i][:], ALU.add)
-        for i in range(PIECES):
-            nc.vector.tensor_scalar_max(rise[:, span[i]], full[i][:], 0.0)
-        nc.vector.tensor_tensor(c0[:].indirect(h0_t[:]), g0[:], rise[:], ALU.add)
-        nc.sync.dma_start(out, c0[:])
+        for h in range(HALVES):
+            nc.vector.tensor_tensor(
+                diff2[h][:], row2[:].indirect(h2_list[:, columns[h]]), g0[:, entries[h]], ALU.subtract
+            )
+
+        gap = halves("gap", F32)
+        gap_plus_y = halves("gap_plus_y", F32)
+        excess = halves("excess", F32)
+        rise = keep.tile([P, S], F32, name="rise")
+        for h in range(HALVES):
+            nc.vector.scalar_tensor_tensor(gap[h][:], diff1[h][:], 0.0, diff2[h][:], ALU.min, ALU.min)
+        for h in range(HALVES):
+            nc.vector.scalar_tensor_tensor(gap_plus_y[h][:], y[h][:], 0.0, gap[h][:], ALU.max, ALU.add)
+        for h in range(HALVES):
+            nc.vector.tensor_tensor(excess[h][:], gap_plus_y[h][:], log_term[h][:], ALU.add)
+        for h in range(HALVES):
+            nc.vector.tensor_scalar_max(rise[:, entries[h]], excess[h][:], 0.0)
+
+        nc.vector.tensor_tensor(row0[:].indirect(h0_list[:]), g0[:], rise[:], ALU.add)
+        nc.sync.dma_start(out, row0[:])

from contextlib import ExitStack

import concourse.mybir as mybir

K, T, S, N, U = 512, 2048, 512, 128, 1024
FLOPS = 2 * K * N * S

F32 = mybir.dt.float32
BF16 = mybir.dt.bfloat16
I32 = mybir.dt.int32
U32 = mybir.dt.uint32
U16 = mybir.dt.uint16
U8 = mybir.dt.uint8
FP8X4 = mybir.dt.float8_e4m3fn_x4
ALU = mybir.AluOpType
ACT = mybir.ActivationFunctionType

P = 128
PACK = 4
QUADRANT = 32
SCALE_ROWS = 4
ENTRIES_PER_COLUMN = 16
HALVES = 2
WIDTH = S // HALVES


def tile_picked_ycms2_put_p_kernel(
    tc, x_words, x_scales, w1, cnt0, cnt1, cnt2, offs, hash0, hash1, hash2, out
):
    nc = tc.nc
    list_columns = S // ENTRIES_PER_COLUMN
    half_columns = WIDTH // ENTRIES_PER_COLUMN
    entries = [slice(h * WIDTH, (h + 1) * WIDTH) for h in range(HALVES)]
    columns = [slice(h * half_columns, (h + 1) * half_columns) for h in range(HALVES)]

    with ExitStack() as ctx:
        lists = ctx.enter_context(tc.tile_pool(name="lists", bufs=1))
        keep = ctx.enter_context(tc.tile_pool(name="keep", bufs=1))
        psum = ctx.enter_context(tc.psum_pool(name="psum", bufs=1))

        def halves(name, dtype):
            return [keep.tile([P, WIDTH], dtype, name=f"{name}{h}", align_bytes=64) for h in range(HALVES)]

        idx_list = lists.tile([P, list_columns], U16, name="idx_list")
        h0_list = lists.tile([P, list_columns], U16, name="h0_list")
        h1_list = lists.tile([P, list_columns], U16, name="h1_list")
        h2_list = lists.tile([P, list_columns], U16, name="h2_list")

        all_words = keep.tile([P, T], I32, name="all_words", align_bytes=64)
        all_scales = keep.tile([P, T], U8, name="all_scales", align_bytes=64)
        w_raw = keep.tile([P, PACK, N], F32, name="w_raw", align_bytes=64)
        row0 = keep.tile([P, U], F32, name="row0", align_bytes=64)
        row1 = keep.tile([P, U], F32, name="row1", align_bytes=64)
        row2 = keep.tile([P, U], F32, name="row2", align_bytes=64)

        nc.vector.memset(all_scales[:].bitcast(I32), 0)

        nc.sync.dma_start(idx_list[:], offs)
        nc.sync.dma_start(w_raw[:], w1.rearrange("(p t) n -> p t n", t=PACK))
        nc.sync.dma_start(h0_list[:], hash0)
        for q in range(P // QUADRANT):
            nc.sync.dma_start(
                all_scales[QUADRANT * q : QUADRANT * q + SCALE_ROWS, :].bitcast(I32),
                x_scales[0, SCALE_ROWS * q : SCALE_ROWS * (q + 1), :].bitcast(I32),
            )
        nc.sync.dma_start(all_words[:], x_words[0].rearrange("p c t -> p (c t)").bitcast(I32))
        nc.sync.dma_start(row0[:], cnt0)
        nc.sync.dma_start(h1_list[:], hash1)
        nc.sync.dma_start(row1[:], cnt1)
        nc.sync.dma_start(h2_list[:], hash2)
        nc.sync.dma_start(row2[:], cnt2)

        w_bf16 = keep.tile([P, N, PACK], BF16, name="w_bf16", align_bytes=64)
        w_words = keep.tile([P, N], U32, name="w_words", align_bytes=64)
        w_scales = keep.tile([P, N], U8, name="w_scales", align_bytes=64)
        nc.scalar.activation(w_bf16[:], w_raw[:].rearrange("p t n -> p n t"), ACT.Copy)
        nc.vector.quantize_mx(
            out=w_words[:].bitcast(FP8X4),
            scales=w_scales[:],
            in_=w_bf16[:].rearrange("p n t -> p (n t)"),
        )

        picked_scales = keep.tile([P, S], U8, name="picked_scales", align_bytes=64)
        picked_words = halves("picked_words", U32)
        nc.vector.tensor_copy(picked_scales[:], all_scales[:].indirect(idx_list[:]))
        for h in range(HALVES):
            nc.vector.tensor_copy(picked_words[h][:], all_words[:].bitcast(U32).indirect(idx_list[:, columns[h]]))

        y = [psum.tile([P, WIDTH], F32, name=f"y{h}") for h in range(HALVES)]
        y_abs = halves("y_abs", F32)
        decay = halves("decay", F32)
        log_term = halves("log_term", F32)
        for h in range(HALVES):
            nc.tensor.matmul_mx(
                out=y[h][:],
                lhsT=w_words[:].bitcast(FP8X4),
                lhsT_scale=w_scales[:],
                rhs=picked_words[h][:].bitcast(FP8X4),
                rhs_scale=picked_scales[:, entries[h]],
                start=True,
                stop=True,
            )
            nc.scalar.activation(y_abs[h][:], y[h][:], ACT.Abs)
            nc.scalar.activation(decay[h][:], y_abs[h][:], ACT.Exp, scale=-1.0)
        for h in range(HALVES):
            nc.scalar.activation(log_term[h][:], decay[h][:], ACT.Ln, bias=1.0)

        g0 = keep.tile([P, S], F32, name="g0")
        diff1 = halves("diff1", F32)
        diff2 = halves("diff2", F32)
        for h in range(HALVES):
            nc.vector.tensor_copy(g0[:, entries[h]], row0[:].indirect(h0_list[:, columns[h]]))
        for h in range(HALVES):
            nc.vector.tensor_tensor(
                diff1[h][:], row1[:].indirect(h1_list[:, columns[h]]), g0[:, entries[h]], ALU.subtract
            )
        for h in range(HALVES):
            nc.vector.tensor_tensor(
                diff2[h][:], row2[:].indirect(h2_list[:, columns[h]]), g0[:, entries[h]], ALU.subtract
            )

        gap = halves("gap", F32)
        gap_plus_y = halves("gap_plus_y", F32)
        excess = halves("excess", F32)
        rise = keep.tile([P, S], F32, name="rise")
        for h in range(HALVES):
            nc.vector.scalar_tensor_tensor(gap[h][:], diff1[h][:], 0.0, diff2[h][:], ALU.min, ALU.min)
        for h in range(HALVES):
            nc.vector.scalar_tensor_tensor(gap_plus_y[h][:], y[h][:], 0.0, gap[h][:], ALU.max, ALU.add)
        for h in range(HALVES):
            nc.vector.tensor_tensor(excess[h][:], gap_plus_y[h][:], log_term[h][:], ALU.add)
        for h in range(HALVES):
            nc.vector.tensor_scalar_max(rise[:, entries[h]], excess[h][:], 0.0)

        nc.vector.tensor_tensor(row0[:].indirect(h0_list[:]), g0[:], rise[:], ALU.add)
        nc.sync.dma_start(out, row0[:])
